import numpy as np
import ml_dtypes


def mxq(x, axis, fmt="e4m3"):
    dtype, down = {"e4m3": (ml_dtypes.float8_e4m3fn, 7), "e5m2": (ml_dtypes.float8_e5m2, 14)}[fmt]
    v = np.moveaxis(np.asarray(x, np.float32).astype(ml_dtypes.bfloat16).astype(np.float64), axis, -1)
    blocks = v.reshape(v.shape[:-1] + (-1, 32))
    amax = np.abs(blocks).max(-1, keepdims=True)
    byte = np.maximum(np.where(amax > 0, np.frexp(amax)[1] - 1 + 127, 0) - down, 1)
    scale = np.exp2(byte - 127.0)
    codes = (blocks / scale).astype(np.float32).astype(dtype).astype(np.float64)
    return np.moveaxis((codes * scale).reshape(v.shape), -1, axis)


WIDE = False


def mx_kscale(k):
    if not WIDE:
        return np.ones(k)
    levels = np.array([10, -10, 5, -5, 0])
    if k % 512:
        return np.exp2(np.random.permutation(np.resize(levels, k // 32))).repeat(32)
    a = np.empty((k // 512, 16))
    for p in range(k // 512):
        a[p, :8] = np.random.permutation(np.resize(levels, 8))
        for g in range(8):
            far = levels[np.abs(levels - a[p, g]) >= 10]
            a[p, g + 8] = far[np.random.randint(len(far))]
    return np.exp2(a.ravel()).repeat(32)


BF16 = ml_dtypes.bfloat16


def bf(x):
    return np.asarray(x, np.float32).astype(BF16)


def f64(x):
    return np.asarray(x).astype(np.float64)


E2M1 = np.array([0.0, 0.5, 1.0, 1.5, 2.0, 3.0, 4.0, 6.0, -0.0, -0.5, -1.0, -1.5, -2.0, -3.0, -4.0, -6.0])


def pack_weight(w, fmt):
    k, n = w.shape
    w = f64(bf(w)).reshape(k // 32, 32, n)
    amax = np.abs(w).max(1)
    if fmt == "e4m3":
        byte = np.frexp(amax)[1] - 1 + 127 - 7
    else:
        mant, ex = np.frexp(amax / 6.0)
        byte = np.where(mant > 0.5, ex, ex - 1) + 127
    byte = np.clip(np.where(amax > 0, byte, 1), 1, 254)
    scaled = (w * np.exp2(127.0 - byte)[:, None, :]).reshape(k, n).astype(np.float32)
    by_word = np.ascontiguousarray(scaled.reshape(k // 512, 128, 4, n).transpose(0, 1, 3, 2))
    if fmt == "e4m3":
        words = by_word.astype(ml_dtypes.float8_e4m3fn).view(np.uint8)
    else:
        c = by_word.astype(ml_dtypes.float4_e2m1fn).view(np.uint8) & 0xF
        words = c[..., 0::2] | (c[..., 1::2] << 4)
    return np.ascontiguousarray(words), np.ascontiguousarray(byte.astype(np.uint8).reshape(k // 512, 16, n))


def unpack_weight(words, scales, fmt):
    g, p, n, _ = words.shape
    if fmt == "e4m3":
        vals = np.ascontiguousarray(words).view(ml_dtypes.float8_e4m3fn).astype(np.float64)
    else:
        nib = np.empty((g, p, n, 4), np.uint8)
        nib[..., 0::2] = words & 0xF
        nib[..., 1::2] = words >> 4
        vals = E2M1[nib]
    vals = vals * np.repeat(np.exp2(scales.astype(np.float64) - 127.0), 8, axis=1)[..., None]
    return vals.transpose(0, 1, 3, 2).reshape(g * 512, n)
def pack4(w):
    words, scales = pack_weight(w, "e2m1")
    return words.reshape(words.shape[0], 128, -1), scales


def unpack4(words, scales):
    return unpack_weight(words.reshape(words.shape[0], 128, -1, 2), scales, "e2m1")


B, U, V, H, W = 4, 1024, 1024, 512, 512


def setup_inputs():
    s, t = mx_kscale(V), mx_kscale(U)
    cx = np.random.standard_normal((V, W)) / np.sqrt(V) / s[:, None]
    cy = np.random.standard_normal((U, H)) / np.sqrt(U) / t[:, None]
    cx_words, cx_scales = pack4(cx)
    cy_words, cy_scales = pack_weight(cy, "e4m3")
    return {"x": bf(np.random.standard_normal((B, U, V))),
            "transfer": bf((1 + 0.1 * np.random.standard_normal((U, V))) * s),
            "cx_words": cx_words, "cx_scales": cx_scales,
            "noise": bf(0.5 * np.exp(0.3 * np.random.standard_normal(U))),
            "gain": bf((1 + 0.1 * np.random.standard_normal(U)) * t),
            "cy_words": cy_words, "cy_scales": cy_scales,
            "background": bf(0.3 * np.random.standard_normal((H, W)))}


def reference(x, transfer, cx_words, cx_scales, noise, gain, cy_words, cy_scales, background):
    f = f64(x) * f64(transfer)
    r = mxq(f, 2, "e4m3").reshape(B * U, V) @ unpack4(cx_words, cx_scales)
    r = r.reshape(B, U, W)
    e = r * r
    d = f64(gain)[:, None] * (r * (e / (e + f64(noise)[:, None])))
    z = unpack_weight(cy_words, cy_scales, "e4m3").T @ mxq(d, 1, "e4m3").transpose(1, 0, 2).reshape(U, B * W)
    return z.reshape(H, B, W).transpose(1, 0, 2) + f64(background)

from contextlib import ExitStack

import concourse.mybir as mybir
from concourse.masks import make_identity

B, U, V, H, W = 4, 1024, 1024, 512, 512
FLOPS = 2 * B * U * V * W + 2 * B * U * H * W

F32 = mybir.dt.float32
BF16 = mybir.dt.bfloat16
U32 = mybir.dt.uint32
I32 = mybir.dt.int32
U8 = mybir.dt.uint8
FP8X4 = mybir.dt.float8_e4m3fn_x4
FP4X4 = mybir.dt.float4_e2m1fn_x4
ACT = mybir.ActivationFunctionType
ALU = mybir.AluOpType

P = 128
NSLOT = 32


def tile_dct_filter_synthesis_f7_kernel(
    tc, x, transfer, cx_words, cx_scales, noise, gain, cy_words, cy_scales, background, out
):
    nc = tc.nc
    with ExitStack() as ctx:
        keep = ctx.enter_context(tc.tile_pool(name="keep", bufs=1))
        xpool = ctx.enter_context(tc.tile_pool(name="xpool", bufs=7))
        work = ctx.enter_context(tc.tile_pool(name="work", bufs=2))
        psum = ctx.enter_context(tc.psum_pool(name="psum", bufs=2))

        ident = keep.tile([P, P], F32)
        planes = keep.tile([P, 4, 512], U8, align_bytes=64)
        cx = keep.tile([P, 2, 1024], U8, align_bytes=64)
        cy = keep.tile([P, 2, 512], U32, align_bytes=64)
        bg = keep.tile([P, 4, 512], BF16)
        noise_raw = keep.tile([P, 8], BF16)
        gain_raw = keep.tile([P, 8], BF16)
        noise_u = keep.tile([P, 8], F32)
        gain_u = keep.tile([P, 8], F32)
        spare = keep.tile([P, 2], F32)
        gate = keep.tile([P, 64], U8)
        tr_raw = keep.tile([P, 2, 4, 1024], BF16)
        tr_t = keep.tile([P, 8, 1024], BF16)

        ctx.enter_context(tc.manual_schedule())

        nc.vector.memset(planes[:].rearrange("p g n -> p (g n)").bitcast(I32), 0)
        nc.vector.memset(spare[:], 1.0)
        nc.scalar.activation(out=spare[:, 1:2], in_=spare[:, 0:1], func=ACT.Abs_reciprocal_sqrt)
        make_identity(nc, ident[:])

        tr_view = [
            transfer[512 * h : 512 * (h + 1), :].rearrange("(p t) v -> p t v", t=4) for h in range(2)
        ]
        xs = {}

        def load_rows(b, h, t0, t1):
            if t0 == 0:
                xt = xpool.tile([P, 4, 1024], BF16, name="xt")
                xs[(b, h)] = xt
            if b == 0:
                nc.sync.dma_start(out=tr_raw[:, h, t0:t1, :], in_=tr_view[h][:, t0:t1, :])
            view = x[b, 512 * h : 512 * (h + 1), :].rearrange("(p t) v -> p t v", t=4)
            nc.sync.dma_start(out=xs[(b, h)][:, t0:t1, :], in_=view[:, t0:t1, :])

        def load_scales(scales, row):
            for q in range(4):
                nc.sync.dma_start(
                    out=planes[32 * q : 32 * q + 4, row : row + 2, :].bitcast(I32),
                    in_=scales[:, 4 * q : 4 * q + 4, :].rearrange("g r n -> r g n").bitcast(I32),
                )

        load_rows(0, 0, 0, 1)
        nc.sync.dma_start(out=cx[:].bitcast(I32), in_=cx_words.rearrange("g p n -> p g n").bitcast(I32))
        load_scales(cx_scales, 0)
        load_rows(0, 0, 1, 2)
        for raw, vec in ((noise_raw, noise), (gain_raw, gain)):
            nc.sync.dma_start(
                out=raw[:].rearrange("p (h t) -> p h t", h=2),
                in_=vec.rearrange("(h p t) -> p h t", h=2, t=4),
            )
        nc.gpsimd.tensor_copy(out=noise_u[:], in_=noise_raw[:])
        nc.gpsimd.tensor_copy(out=gain_u[:], in_=gain_raw[:])
        load_rows(0, 0, 2, 4)
        load_rows(0, 1, 0, 2)
        load_rows(0, 1, 2, 4)
        load_rows(1, 0, 0, 4)
        load_rows(1, 1, 0, 4)
        load_scales(cy_scales, 2)
        nc.sync.dma_start(
            out=cy[:].bitcast(I32), in_=cy_words.rearrange("g p n t -> p g (n t)").bitcast(I32)
        )
        nc.sync.dma_start(out=bg[:], in_=background.rearrange("(m p) j -> p m j", p=P))
        for b, h in ((2, 0), (2, 1), (3, 0), (3, 1)):
            load_rows(b, h, 0, 4)

        x_turned = {}
        f_bf = {}
        f_q = {}
        r_ps = {}
        ew = {}
        d_bf = {}
        d_q = {}
        z_ps = {}
        outs = {}

        def turn(src):
            bank = psum.tile([P, 2, 2, P], F32, name="bank_t", bufs=3)
            words = src.bitcast(F32)
            for g in range(2):
                for w in range(2):
                    nc.tensor.transpose(
                        bank[:, w, g, :], words[:, 256 * g + w : 256 * (g + 1) : 2], ident[:]
                    )
            return bank

        def where(s):
            return s // 8, (s // 4) % 2, s % 4

        def turn_rows(s):
            b, h, t = where(s)
            if b == 0:
                bank = turn(tr_raw[:, h, t, :])
                nc.scalar.copy(
                    out=tr_t[:, 4 * h + t, :].bitcast(F32).rearrange("p (w u) -> p w u", u=2),
                    in_=bank[:].rearrange("p u g r -> p (g r) u"),
                )
            x_turned[s] = turn(xs[(b, h)][:, t, :])

        def multiply(s):
            b, h, t = where(s)
            bank = x_turned[s]
            f = work.tile([P, 1024], BF16, name="f", bufs=4, align_bytes=64)
            nc.vector.tensor_tensor(
                out=f[:].rearrange("p (w u e) -> p w u e", u=2, e=2),
                in0=bank[:].rearrange("p u g r -> p (u g r)").bitcast(BF16).rearrange(
                    "p (u w e) -> p w u e", u=2, e=2
                ),
                in1=tr_t[:, 4 * h + t, :].rearrange("p (w u e) -> p w u e", u=2, e=2),
                op=ALU.mult,
            )
            f_bf[s] = f

        def quantize_f(s):
            codes = work.tile([P, 256], U32, name="f_codes", bufs=4, align_bytes=64)
            scales = work.tile([P, 256], U8, name="f_scales", bufs=4, align_bytes=64)
            nc.vector.quantize_mx(out=codes[:].bitcast(FP8X4), scales=scales[:], in_=f_bf[s][:])
            f_q[s] = codes, scales

        def synth_rows(s):
            codes, scales = f_q[s]
            bank = psum.tile([P, 512], F32, name="bank_r", bufs=3)
            for g in range(2):
                nc.tensor.matmul_mx(
                    out=bank[:],
                    lhsT=codes[:, P * g : P * (g + 1)].bitcast(FP8X4),
                    lhsT_scale=scales[:, P * g : P * (g + 1)],
                    rhs=cx[:, g, :].bitcast(FP4X4),
                    rhs_scale=planes[:, g, :],
                    start=(g == 0),
                    stop=(g == 1),
                )
            r_ps[s] = bank

        def square(s):
            b, h, t = where(s)
            if t == 0:
                e = work.tile([P, 4, 512], F32, name="e")
                w = work.tile([P, 4, 512], F32, name="w", bufs=3)
                c = work.tile([P, 4, 512], F32, name="c", bufs=3)
                ew[s // 4] = e, w, c
            e, w, c = ew[s // 4]
            nc.scalar.activation(out=e[:, t, :], in_=r_ps[s][:], func=ACT.Square)

        def cube(s):
            b, h, t = where(s)
            e, w, c = ew[s // 4]
            nc.vector.scalar_tensor_tensor(
                out=c[:, t, :],
                in0=r_ps[s][:],
                scalar=gain_u[:, 4 * h + t : 4 * h + t + 1],
                in1=e[:, t, :],
                op0=ALU.mult,
                op1=ALU.mult,
            )

        def inv_root(s):
            b, h, t = where(s)
            e, w, c = ew[s // 4]
            nc.scalar.activation(
                out=w[:, t, :],
                in_=e[:, t, :],
                func=ACT.Abs_reciprocal_sqrt,
                bias=noise_u[:, 4 * h + t : 4 * h + t + 1],
            )

        def inv(s):
            t = s % 4
            e, w, c = ew[s // 4]
            nc.scalar.activation(out=w[:, t, :], in_=w[:, t, :], func=ACT.Square)

        def shrink(k, q):
            e, w, c = ew[k]
            if q == 0:
                dt = work.tile([P, 512, 4], BF16, name="d", align_bytes=64)
                d_bf[k] = dt
            cols = slice(P * q, P * (q + 1))
            engine = nc.vector if k >= 6 else nc.gpsimd
            engine.tensor_tensor(
                out=d_bf[k][:, cols, :].rearrange("p (c i) t -> p c t i", i=2),
                in0=c[:, :, cols].rearrange("p t (c i) -> p c t i", i=2),
                in1=w[:, :, cols].rearrange("p t (c i) -> p c t i", i=2),
                op=ALU.mult,
            )

        def quantize_d(k, q):
            if q == 0:
                codes = work.tile([P, 512], U32, name="d_codes", bufs=4, align_bytes=64)
                scales = work.tile([P, 512], U8, name="d_scales", bufs=4, align_bytes=64)
                d_q[k] = codes, scales
            codes, scales = d_q[k]
            cols = slice(P * q, P * (q + 1))
            nc.vector.quantize_mx(
                out=codes[:, cols].bitcast(FP8X4),
                scales=scales[:, cols],
                in_=d_bf[k][:, cols, :].rearrange("p j t -> p (j t)"),
            )

        def synth_cols(b, m):
            bank = psum.tile([P, 512], F32, name="bank_z")
            for h in range(2):
                codes, scales = d_q[2 * b + h]
                nc.tensor.matmul_mx(
                    out=bank[:],
                    lhsT=cy[:, h, P * m : P * (m + 1)].bitcast(FP8X4),
                    lhsT_scale=planes[:, 2 + h, P * m : P * (m + 1)],
                    rhs=codes[:].bitcast(FP8X4),
                    rhs_scale=scales[:],
                    start=(h == 0),
                    stop=(h == 1),
                )
            z_ps[(b, m)] = bank

        def finish(b, m):
            if m == 0:
                o = work.tile([P, 4, 512], F32, name="o")
                outs[b] = o
            o = outs[b]
            nc.vector.tensor_tensor(out=o[:, m, :], in0=z_ps[(b, m)][:], in1=bg[:, m, :], op=ALU.add)
            nc.sync.dma_start(
                out=out[b].rearrange("(m p) j -> p m j", p=P)[:, m, :], in_=o[:, m, :]
            )

        for s in range(NSLOT + 20):
            if s < NSLOT:
                turn_rows(s)
            last_scales = None
            i = s - 1
            if 0 <= i < NSLOT:
                quantize_f(i)
                last_scales = f_q[i][1][:, 0:1]
            i = s - 11
            if 0 <= i < NSLOT:
                quantize_d(i // 4, i % 4)
                last_scales = d_q[i // 4][1][:, P * (i % 4) : P * (i % 4) + 1]
            i = s - 3
            if 0 <= i < NSLOT:
                synth_rows(i)
            i = s - 18
            if 0 <= i < NSLOT and i % 2 == 1:
                synth_cols(i // 8, (i % 8) // 2)
            i = s - 5
            if 0 <= i < NSLOT:
                inv(i)
            i = s - 4
            if 0 <= i < NSLOT:
                inv_root(i)
            i = s - 3
            if 0 <= i < NSLOT:
                square(i)
            if s < NSLOT:
                multiply(s)
            i = s - 4
            if 0 <= i < NSLOT:
                cube(i)
            i = s - 9
            if 0 <= i < NSLOT:
                if i < 24 and last_scales is not None:
                    nc.gpsimd.tensor_copy(out=gate[:, 0:1], in_=last_scales)
                shrink(i // 4, i % 4)
            i = s - 19
            if 0 <= i < NSLOT and i % 2 == 1:
                finish(i // 8, (i % 8) // 2)
